import numpy as np
import ml_dtypes


def mxq(x, axis, fmt="e4m3"):
    dtype, down = {"e4m3": (ml_dtypes.float8_e4m3fn, 7), "e5m2": (ml_dtypes.float8_e5m2, 14)}[fmt]
    v = np.moveaxis(np.asarray(x, np.float32).astype(ml_dtypes.bfloat16).astype(np.float64), axis, -1)
    blocks = v.reshape(v.shape[:-1] + (-1, 32))
    amax = np.abs(blocks).max(-1, keepdims=True)
    byte = np.maximum(np.where(amax > 0, np.frexp(amax)[1] - 1 + 127, 0) - down, 1)
    scale = np.exp2(byte - 127.0)
    codes = (blocks / scale).astype(np.float32).astype(dtype).astype(np.float64)
    return np.moveaxis((codes * scale).reshape(v.shape), -1, axis)


WIDE = False


def mx_kscale(k):
    if not WIDE:
        return np.ones(k)
    levels = np.array([10, -10, 5, -5, 0])
    if k % 512:
        return np.exp2(np.random.permutation(np.resize(levels, k // 32))).repeat(32)
    a = np.empty((k // 512, 16))
    for p in range(k // 512):
        a[p, :8] = np.random.permutation(np.resize(levels, 8))
        for g in range(8):
            far = levels[np.abs(levels - a[p, g]) >= 10]
            a[p, g + 8] = far[np.random.randint(len(far))]
    return np.exp2(a.ravel()).repeat(32)


def f64(x):
    return np.asarray(x).astype(np.float64)


def striped(idx):
    return np.tile(idx.reshape(-1, 16).T, (8, 1)).astype(np.uint16)


def unstriped(offs):
    return offs[:16].T.reshape(-1).astype(np.int64)


E2M1 = np.array([0.0, 0.5, 1.0, 1.5, 2.0, 3.0, 4.0, 6.0, -0.0, -0.5, -1.0, -1.5, -2.0, -3.0, -4.0, -6.0])


def pack_weight(w, fmt):
    k, n = w.shape
    w = f64(np.asarray(w, np.float32).astype(ml_dtypes.bfloat16)).reshape(k // 32, 32, n)
    amax = np.abs(w).max(1)
    if fmt == "e4m3":
        byte = np.frexp(amax)[1] - 1 + 127 - 7
    else:
        mant, ex = np.frexp(amax / 6.0)
        byte = np.where(mant > 0.5, ex, ex - 1) + 127
    byte = np.clip(np.where(amax > 0, byte, 1), 1, 254)
    scaled = (w * np.exp2(127.0 - byte)[:, None, :]).reshape(k, n).astype(np.float32)
    by_word = np.ascontiguousarray(scaled.reshape(k // 512, 128, 4, n).transpose(0, 1, 3, 2))
    if fmt == "e4m3":
        words = by_word.astype(ml_dtypes.float8_e4m3fn).view(np.uint8)
    else:
        c = by_word.astype(ml_dtypes.float4_e2m1fn).view(np.uint8) & 0xF
        words = (c[..., 0::2] | (c[..., 1::2] << 4)).reshape(k // 512, 128, 2 * n)
    return np.ascontiguousarray(words), np.ascontiguousarray(byte.astype(np.uint8).reshape(k // 512, 16, n))


def unpack_weight(words, scales, fmt):
    g, _, n = scales.shape
    words = np.ascontiguousarray(words).reshape(g, 128, n, -1)
    if fmt == "e4m3":
        vals = words.view(ml_dtypes.float8_e4m3fn).astype(np.float64)
    else:
        nib = np.empty((g, 128, n, 4), np.uint8)
        nib[..., 0::2] = words & 0xF
        nib[..., 1::2] = words >> 4
        vals = E2M1[nib]
    vals = vals * np.repeat(np.exp2(scales.astype(np.float64) - 127.0), 8, axis=1)[..., None]
    return vals.transpose(0, 1, 3, 2).reshape(g * 512, n)


K, T, E, C, N = 128, 1024, 12, 256, 512
TOP = 3


def by_expert(wq, xq):
    return np.concatenate([wq[e].T @ xq[:, e * C:(e + 1) * C] for e in range(E)], axis=1)


def setup_inputs():
    n = np.random.standard_normal
    s = mx_kscale(N)[:, None]
    deal = np.repeat(np.arange(E), C).reshape(TOP, T)[:, np.random.permutation(T)]
    deal = np.take_along_axis(deal, np.argsort(np.random.rand(TOP, T), axis=0), axis=0)
    for _ in range(8):
        s_, t_ = np.random.permutation(T).reshape(2, -1); r = np.random.randint(TOP, size=T // 2); x, y = deal[r, s_].copy(), deal[r, t_].copy()
        ok = ~((deal[:, s_] == y).any(0) | (deal[:, t_] == x).any(0)); deal[r[ok], s_[ok]] = y[ok]; deal[r[ok], t_[ok]] = x[ok]
    order = np.lexsort((np.random.rand(TOP * T), deal.reshape(-1)))
    slot_token = order % T; pos = np.empty(TOP * T, np.int64); pos[order] = np.arange(TOP * T); pos = pos.reshape(TOP, T)
    g = np.random.uniform(0.5, 1.5, (TOP, T)); g = g / g.sum(0)
    w_slot = np.empty(E * C)
    for r in range(TOP): w_slot[pos[r]] = g[r]
    dy = pack_weight(n((N, T)) * s, "e4m3")
    return {
        "dy_words": dy[0],
        "dy_scales": dy[1],
        "w": (n((E + 1, N, K)) / np.sqrt(N) / s[None]).astype(np.float32),
        "gate": np.tile(w_slot, (K, 1)).astype(np.float32),
        "offs": striped(slot_token),
        "pos1": striped(pos[0]),
        "pos2": striped(pos[1]),
        "pos3": striped(pos[2]),
    }


def reference(dy_words, dy_scales, w, gate, offs, pos1, pos2, pos3):
    idx = unstriped(offs)
    gq = unpack_weight(dy_words, dy_scales, "e4m3")[:, idx]
    wq = mxq(f64(w), 1, "e4m3")
    ds = wq[E].T @ unpack_weight(dy_words, dy_scales, "e4m3")
    dx = f64(gate) * by_expert(wq, gq)
    return ds + dx[:, unstriped(pos1)] + dx[:, unstriped(pos2)] + dx[:, unstriped(pos3)]

@@ -1,0 +1,190 @@
+from contextlib import ExitStack
+
+import concourse.mybir as mybir
+from concourse.masks import make_identity
+
+K, T, E, C, N = 128, 1024, 12, 256, 512
+S = E * C
+P = 128
+FLOPS = 2 * N * K * (S + T)
+
+F32 = mybir.dt.float32
+BF16 = mybir.dt.bfloat16
+I32 = mybir.dt.int32
+U32 = mybir.dt.uint32
+U16 = mybir.dt.uint16
+U8 = mybir.dt.uint8
+FP8X4 = mybir.dt.float8_e4m3fn_x4
+COPY = mybir.ActivationFunctionType.Copy
+MULT = mybir.AluOpType.mult
+ADD = mybir.AluOpType.add
+
+BANK = 512
+TURNED = 10
+
+
+def tile_moe_bds_lin_none_kernel(tc, dy_words, dy_scales, w, gate, offs, pos1, pos2, pos3, out):
+    nc = tc.nc
+    with ExitStack() as ctx:
+        keep = ctx.enter_context(tc.tile_pool(name="keep", bufs=1))
+        ring = ctx.enter_context(tc.tile_pool(name="ring", bufs=2))
+        psum = ctx.enter_context(tc.psum_pool(name="psum", bufs=2))
+
+        offs_t = keep.tile([P, S // 16], U16, name="offs_t")
+        pos_t = [keep.tile([P, T // 16], U16, name="pos%d_t" % r) for r in range(3)]
+        tok_words = keep.tile([P, T], I32, name="tok_words", align_bytes=64)
+        tok_scales = keep.tile([P, T], U8, name="tok_scales", align_bytes=64)
+        slot_words = keep.tile([P, S], U32, name="slot_words", align_bytes=64)
+        slot_scales = keep.tile([P, S], U8, name="slot_scales", align_bytes=64)
+        w_raw = keep.tile([P, E + 1, 4, K], F32, name="w_raw")
+        w_bf = keep.tile([P, E + 1, K, 4], BF16, name="w_bf", align_bytes=64)
+        w_codes = keep.tile([P, (E + 1) * K], U32, name="w_codes", align_bytes=64)
+        w_scales = keep.tile([P, (E + 1) * K], U8, name="w_scales", align_bytes=64)
+        gate_rows = keep.tile([P, P], F32, name="gate_rows")
+        gate_cols = keep.tile([P, 2 * TURNED], F32, name="gate_cols")
+        gate_tail = keep.tile([P, (E - TURNED) * C], F32, name="gate_tail")
+        dx = keep.tile([P, S], F32, name="dx")
+        ds = keep.tile([P, T], F32, name="ds")
+        picked = [keep.tile([P, T], F32, name="picked%d" % r) for r in range(3)]
+        result = keep.tile([P, T], F32, name="result")
+        made = keep.tile([P, P], F32, name="made")
+        ident = keep.tile([P, P], F32, name="ident")
+
+        nc.vector.memset(tok_scales[:].bitcast(I32), 0)
+        make_identity(nc, made[:])
+        nc.scalar.activation(ident[:], made[:], COPY)
+
+        def load_w(e0, e1):
+            nc.sync.dma_start(
+                w_raw[:, e0:e1].rearrange("p e t k -> p e (t k)"),
+                w[e0:e1].rearrange("e (p t) k -> p e (t k)", t=4),
+            )
+
+        nc.sync.dma_start(offs_t[:], offs)
+        for q in range(4):
+            nc.sync.dma_start(tok_scales[32 * q : 32 * q + 4, :].bitcast(I32), dy_scales[0, 4 * q : 4 * q + 4, :].bitcast(I32))
+        load_w(0, 1)
+        load_w(1, 2)
+        load_w(2, 4)
+        load_w(4, 6)
+        nc.sync.dma_start(tok_words[:], dy_words[0].rearrange("p t d -> p (t d)").bitcast(I32))
+        nc.sync.dma_start(gate_rows[:], gate.rearrange("k (b s) -> (k b) s", s=P)[0:P, :])
+        load_w(6, 8)
+        load_w(8, 10)
+        load_w(10, 12)
+        nc.sync.dma_start(gate_tail[:], gate[:, TURNED * C :])
+        load_w(12, 13)
+        for r, pos in enumerate((pos1, pos2, pos3)):
+            nc.sync.dma_start(pos_t[r][:], pos)
+
+        def cast_w(e):
+            nc.scalar.copy(
+                w_bf[:, e].rearrange("p (c i) t -> p c t i", i=4),
+                w_raw[:, e].rearrange("p t (c i) -> p c t i", i=4),
+            )
+
+        def quantize_w(e0, e1):
+            nc.vector.quantize_mx(
+                out=w_codes[:, e0 * K : e1 * K].bitcast(FP8X4),
+                scales=w_scales[:, e0 * K : e1 * K],
+                in_=w_bf[:, e0:e1].rearrange("p e k t -> p (e k t)"),
+            )
+
+        def gather_words(s0, s1):
+            nc.vector.tensor_copy(slot_words[:, s0:s1], tok_words[:].bitcast(U32).indirect(offs_t[:, s0 // 16 : s1 // 16]))
+
+        def mx(acc, lhs_words, lhs_scales, rhs_words, rhs_scales):
+            nc.tensor.matmul_mx(
+                out=acc, lhsT=lhs_words.bitcast(FP8X4), lhsT_scale=lhs_scales,
+                rhs=rhs_words.bitcast(FP8X4), rhs_scale=rhs_scales, start=True, stop=True,
+            )
+
+        def gather_scales(s0, s1):
+            nc.vector.tensor_copy(slot_scales[:, s0:s1], tok_scales[:].indirect(offs_t[:, s0 // 16 : s1 // 16]))
+
+        for s0 in range(0, 1920, 640):
+            gather_scales(s0, s0 + 640)
+
+        for e in range(6):
+            cast_w(e)
+        gate_ps = psum.tile([P, BANK], F32, name="gate_ps", tag="sum")
+        nc.tensor.transpose(gate_ps[:, 0:P], gate_rows[:], ident[:])
+        nc.scalar.copy(gate_cols[:], gate_ps[:, 0 : 2 * TURNED])
+        for e in range(6, 8):
+            cast_w(e)
+
+        for c in range(TURNED // 2):
+            if c == 2:
+                gather_scales(1920, 2560)
+            if c % 2 == 0:
+                quantize_w(2 * c, 2 * c + 4)
+            s0 = c * BANK
+            gather_words(s0, s0 + BANK)
+            by_slot = psum.tile([P, 4, K], F32, name="by_slot", tag="mx")
+            for j in range(4):
+                b = 4 * c + j
+                e = b // 2
+                mx(by_slot[:, j, :], slot_words[:, b * P : (b + 1) * P], slot_scales[:, b * P : (b + 1) * P],
+                   w_codes[:, e * K : (e + 1) * K], w_scales[:, e * K : (e + 1) * K])
+            gated = ring.tile([P, 4, K], F32, name="gated")
+            for j in range(4):
+                b = 4 * c + j
+                nc.scalar.activation(gated[:, j, :], by_slot[:, j, :], COPY, scale=gate_cols[:, b : b + 1])
+            back = psum.tile([P, BANK], F32, name="back", tag="back")
+            for j in range(4):
+                nc.tensor.transpose(back[:, j * P : (j + 1) * P], gated[:, j, :], ident[:])
+            if c < 2:
+                cast_w(8 + 2 * c)
+                cast_w(9 + 2 * c)
+            nc.scalar.copy(dx[:, s0 : s0 + BANK], back[:])
+
+        gather_scales(TURNED * C, S)
+        cast_w(E)
+        tails = []
+        for e in range(TURNED, E):
+            gather_words(e * C, (e + 1) * C)
+            acc = psum.tile([P, BANK], F32, name="acc", tag="total")
+            mx(acc[:, 0:C], w_codes[:, e * K : (e + 1) * K], w_scales[:, e * K : (e + 1) * K],
+               slot_words[:, e * C : (e + 1) * C], slot_scales[:, e * C : (e + 1) * C])
+            tails.append(acc)
+        for i, e in enumerate(range(TURNED, E)):
+            nc.vector.tensor_tensor(dx[:, e * C : (e + 1) * C], tails[i][:, 0:C], gate_tail[:, i * C : (i + 1) * C], MULT)
+
+        quantize_w(E, E + 1)
+        for h in range(2):
+            cols = slice(h * BANK, (h + 1) * BANK)
+            ds_ps = psum.tile([P, BANK], F32, name="ds_ps", tag="mx")
+            mx(ds_ps[:], w_codes[:, E * K :], w_scales[:, E * K :], tok_words[:, cols], tok_scales[:, cols])
+            nc.scalar.copy(ds[:, cols], ds_ps[:])
+
+        def pick(r, t0, t1):
+            nc.vector.tensor_copy(picked[r][:, t0:t1], dx[:].indirect(pos_t[r][:, t0 // 16 : t1 // 16]))
+
+        sums = [psum.tile([P, 4, K], F32, name="sum%d" % h, tag="sum") for h in range(2)]
+
+        def add_turned(src, h, first, last):
+            for j in range(4):
+                t0 = h * BANK + j * P
+                nc.tensor.matmul(sums[h][:, j, :], src[:, t0 : t0 + P], ident[:], start=(first and j == 0), stop=(last and j == 3), is_transpose=True)
+
+        pick(0, 0, T)
+        for h in range(2):
+            add_turned(ds, h, True, False)
+        for h in range(2):
+            add_turned(picked[0], h, False, False)
+        totals = []
+        for h in range(2):
+            pick(1, h * BANK, (h + 1) * BANK)
+            add_turned(picked[1], h, False, True)
+            by_token = ring.tile([P, 4, K], F32, name="by_token")
+            nc.scalar.copy(by_token[:], sums[h][:])
+            total = psum.tile([P, BANK], F32, name="total", tag="total")
+            for j in range(4):
+                nc.tensor.transpose(total[:, j * P : (j + 1) * P], by_token[:, j, :], ident[:])
+            totals.append(total)
+        for h in range(2):
+            pick(2, h * BANK, (h + 1) * BANK)
+        for h in range(2):
+            cols = slice(h * BANK, (h + 1) * BANK)
+            nc.vector.tensor_tensor(result[:, cols], picked[2][:, cols], totals[h][:], ADD)
+            nc.sync.dma_start(out[:, cols], result[:, cols])

@@ -20,7 +20,7 @@ MULT = mybir.AluOpType.mult
 ADD = mybir.AluOpType.add
 
 BANK = 512
-TURNED = 10
+TURNED = 8
 
 
 def tile_moe_bds_lin_none_kernel(tc, dy_words, dy_scales, w, gate, offs, pos1, pos2, pos3, out):
@@ -34,10 +34,9 @@ def tile_moe_bds_lin_none_kernel(tc, dy_words, dy_scales, w, gate, offs, pos1, p
         pos_t = [keep.tile([P, T // 16], U16, name="pos%d_t" % r) for r in range(3)]
         tok_words = keep.tile([P, T], I32, name="tok_words", align_bytes=64)
         tok_scales = keep.tile([P, T], U8, name="tok_scales", align_bytes=64)
-        slot_words = keep.tile([P, S], U32, name="slot_words", align_bytes=64)
         slot_scales = keep.tile([P, S], U8, name="slot_scales", align_bytes=64)
         w_raw = keep.tile([P, E + 1, 4, K], F32, name="w_raw")
-        w_bf = keep.tile([P, E + 1, K, 4], BF16, name="w_bf", align_bytes=64)
+        w_bf = keep.tile([P, E, K, 4], BF16, name="w_bf", align_bytes=64)
         w_codes = keep.tile([P, (E + 1) * K], U32, name="w_codes", align_bytes=64)
         w_scales = keep.tile([P, (E + 1) * K], U8, name="w_scales", align_bytes=64)
         gate_rows = keep.tile([P, P], F32, name="gate_rows")
@@ -50,9 +49,8 @@ def tile_moe_bds_lin_none_kernel(tc, dy_words, dy_scales, w, gate, offs, pos1, p
         made = keep.tile([P, P], F32, name="made")
         ident = keep.tile([P, P], F32, name="ident")
 
-        nc.vector.memset(tok_scales[:].bitcast(I32), 0)
+        nc.gpsimd.memset(tok_scales[:].bitcast(I32), 0)
         make_identity(nc, made[:])
-        nc.scalar.activation(ident[:], made[:], COPY)
 
         def load_w(e0, e1):
             nc.sync.dma_start(
@@ -62,36 +60,40 @@ def tile_moe_bds_lin_none_kernel(tc, dy_words, dy_scales, w, gate, offs, pos1, p
 
         nc.sync.dma_start(offs_t[:], offs)
         for q in range(4):
-            nc.sync.dma_start(tok_scales[32 * q : 32 * q + 4, :].bitcast(I32), dy_scales[0, 4 * q : 4 * q + 4, :].bitcast(I32))
+            queue = nc.sync if q < 2 else nc.scalar
+            queue.dma_start(tok_scales[32 * q : 32 * q + 4, :].bitcast(I32), dy_scales[0, 4 * q : 4 * q + 4, :].bitcast(I32))
+        nc.scalar.activation(ident[:], made[:], COPY)
         load_w(0, 1)
         load_w(1, 2)
         load_w(2, 4)
         load_w(4, 6)
-        nc.sync.dma_start(tok_words[:], dy_words[0].rearrange("p t d -> p (t d)").bitcast(I32))
-        nc.sync.dma_start(gate_rows[:], gate.rearrange("k (b s) -> (k b) s", s=P)[0:P, :])
         load_w(6, 8)
         load_w(8, 10)
         load_w(10, 12)
+        nc.sync.dma_start(tok_words[:], dy_words[0].rearrange("p t d -> p (t d)").bitcast(I32))
+        nc.sync.dma_start(gate_rows[:], gate.rearrange("k (b s) -> (k b) s", s=P)[0:P, :])
         nc.sync.dma_start(gate_tail[:], gate[:, TURNED * C :])
         load_w(12, 13)
         for r, pos in enumerate((pos1, pos2, pos3)):
             nc.sync.dma_start(pos_t[r][:], pos)
 
-        def cast_w(e):
+        def cast_w(e, dst):
             nc.scalar.copy(
-                w_bf[:, e].rearrange("p (c i) t -> p c t i", i=4),
+                dst.rearrange("p (c i) t -> p c t i", i=4),
                 w_raw[:, e].rearrange("p t (c i) -> p c t i", i=4),
             )
 
-        def quantize_w(e0, e1):
+        def quantize_w(e0, e1, src):
             nc.vector.quantize_mx(
                 out=w_codes[:, e0 * K : e1 * K].bitcast(FP8X4),
                 scales=w_scales[:, e0 * K : e1 * K],
-                in_=w_bf[:, e0:e1].rearrange("p e k t -> p (e k t)"),
+                in_=src,
             )
 
         def gather_words(s0, s1):
-            nc.vector.tensor_copy(slot_words[:, s0:s1], tok_words[:].bitcast(U32).indirect(offs_t[:, s0 // 16 : s1 // 16]))
+            slot_words = ring.tile([P, BANK], U32, name="slot_words", align_bytes=64)
+            nc.vector.tensor_copy(slot_words[:, 0 : s1 - s0], tok_words[:].bitcast(U32).indirect(offs_t[:, s0 // 16 : s1 // 16]))
+            return slot_words
 
         def mx(acc, lhs_words, lhs_scales, rhs_words, rhs_scales):
             nc.tensor.matmul_mx(
@@ -99,61 +101,61 @@ def tile_moe_bds_lin_none_kernel(tc, dy_words, dy_scales, w, gate, offs, pos1, p
                 rhs=rhs_words.bitcast(FP8X4), rhs_scale=rhs_scales, start=True, stop=True,
             )
 
-        def gather_scales(s0, s1):
-            nc.vector.tensor_copy(slot_scales[:, s0:s1], tok_scales[:].indirect(offs_t[:, s0 // 16 : s1 // 16]))
+        for s0 in range(0, S, 768):
+            nc.vector.tensor_copy(slot_scales[:, s0 : s0 + 768], tok_scales[:].indirect(offs_t[:, s0 // 16 : (s0 + 768) // 16]))
 
-        for s0 in range(0, 1920, 640):
-            gather_scales(s0, s0 + 640)
-
-        for e in range(6):
-            cast_w(e)
+        for e in range(E):
+            cast_w(e, w_bf[:, e])
+        for e0 in range(0, E, 4):
+            quantize_w(e0, e0 + 4, w_bf[:, e0 : e0 + 4].rearrange("p e k t -> p (e k t)"))
         gate_ps = psum.tile([P, BANK], F32, name="gate_ps", tag="sum")
         nc.tensor.transpose(gate_ps[:, 0:P], gate_rows[:], ident[:])
         nc.scalar.copy(gate_cols[:], gate_ps[:, 0 : 2 * TURNED])
-        for e in range(6, 8):
-            cast_w(e)
 
         for c in range(TURNED // 2):
-            if c == 2:
-                gather_scales(1920, 2560)
-            if c % 2 == 0:
-                quantize_w(2 * c, 2 * c + 4)
             s0 = c * BANK
-            gather_words(s0, s0 + BANK)
+            words = gather_words(s0, s0 + BANK)
             by_slot = psum.tile([P, 4, K], F32, name="by_slot", tag="mx")
             for j in range(4):
                 b = 4 * c + j
                 e = b // 2
-                mx(by_slot[:, j, :], slot_words[:, b * P : (b + 1) * P], slot_scales[:, b * P : (b + 1) * P],
+                mx(by_slot[:, j, :], words[:, j * P : (j + 1) * P], slot_scales[:, b * P : (b + 1) * P],
                    w_codes[:, e * K : (e + 1) * K], w_scales[:, e * K : (e + 1) * K])
-            gated = ring.tile([P, 4, K], F32, name="gated")
+            gated = ring.tile([P, 4, K], F32, name="gated", tag="gated", align_bytes=64)
             for j in range(4):
                 b = 4 * c + j
                 nc.scalar.activation(gated[:, j, :], by_slot[:, j, :], COPY, scale=gate_cols[:, b : b + 1])
             back = psum.tile([P, BANK], F32, name="back", tag="back")
             for j in range(4):
                 nc.tensor.transpose(back[:, j * P : (j + 1) * P], gated[:, j, :], ident[:])
-            if c < 2:
-                cast_w(8 + 2 * c)
-                cast_w(9 + 2 * c)
             nc.scalar.copy(dx[:, s0 : s0 + BANK], back[:])
 
-        gather_scales(TURNED * C, S)
-        cast_w(E)
-        tails = []
-        for e in range(TURNED, E):
-            gather_words(e * C, (e + 1) * C)
-            acc = psum.tile([P, BANK], F32, name="acc", tag="total")
-            mx(acc[:, 0:C], w_codes[:, e * K : (e + 1) * K], w_scales[:, e * K : (e + 1) * K],
-               slot_words[:, e * C : (e + 1) * C], slot_scales[:, e * C : (e + 1) * C])
-            tails.append(acc)
-        for i, e in enumerate(range(TURNED, E)):
-            nc.vector.tensor_tensor(dx[:, e * C : (e + 1) * C], tails[i][:, 0:C], gate_tail[:, i * C : (i + 1) * C], MULT)
+        def multiply(e0, e1):
+            words = gather_words(e0 * C, e1 * C)
+            acc = psum.tile([P, BANK], F32, name="acc", tag="mx")
+            for e in range(e0, e1):
+                cols = slice((e - e0) * C, (e - e0 + 1) * C)
+                mx(acc[:, cols], w_codes[:, e * K : (e + 1) * K], w_scales[:, e * K : (e + 1) * K],
+                   words[:, cols], slot_scales[:, e * C : (e + 1) * C])
+            return acc
 
-        quantize_w(E, E + 1)
+        def apply_gate(e0, e1, acc):
+            nc.vector.tensor_tensor(dx[:, e0 * C : e1 * C], acc[:, 0 : (e1 - e0) * C],
+                                    gate_tail[:, (e0 - TURNED) * C : (e1 - TURNED) * C], MULT)
+
+        acc0 = multiply(8, 10)
+        acc1 = multiply(10, 11)
+        apply_gate(8, 10, acc0)
+        acc2 = multiply(11, 12)
+        apply_gate(10, 11, acc1)
+        apply_gate(11, 12, acc2)
+
+        shared_bf = ring.tile([P, K, 4], BF16, name="shared_bf", tag="gated", align_bytes=64)
+        cast_w(E, shared_bf[:])
+        quantize_w(E, E + 1, shared_bf[:].rearrange("p k t -> p (k t)"))
         for h in range(2):
             cols = slice(h * BANK, (h + 1) * BANK)
-            ds_ps = psum.tile([P, BANK], F32, name="ds_ps", tag="mx")
+            ds_ps = psum.tile([P, BANK], F32, name="ds_ps", tag="back")
             mx(ds_ps[:], w_codes[:, E * K :], w_scales[:, E * K :], tok_words[:, cols], tok_scales[:, cols])
             nc.scalar.copy(ds[:, cols], ds_ps[:])
 
@@ -184,7 +186,7 @@ def tile_moe_bds_lin_none_kernel(tc, dy_words, dy_scales, w, gate, offs, pos1, p
             totals.append(total)
         for h in range(2):
             pick(2, h * BANK, (h + 1) * BANK)
-        for h in range(2):
-            cols = slice(h * BANK, (h + 1) * BANK)
-            nc.vector.tensor_tensor(result[:, cols], picked[2][:, cols], totals[h][:], ADD)
-            nc.sync.dma_start(out[:, cols], result[:, cols])
+        for t0, t1, queue in ((0, 512, nc.sync), (512, 768, nc.scalar), (768, 1024, nc.sync)):
+            h = t0 // BANK
+            nc.vector.tensor_tensor(result[:, t0:t1], picked[2][:, t0:t1], totals[h][:, t0 - h * BANK : t1 - h * BANK], ADD)
+            queue.dma_start(out[:, t0:t1], result[:, t0:t1])

@@ -36,7 +36,7 @@ def tile_moe_bds_lin_none_kernel(tc, dy_words, dy_scales, w, gate, offs, pos1, p
         tok_scales = keep.tile([P, T], U8, name="tok_scales", align_bytes=64)
         slot_scales = keep.tile([P, S], U8, name="slot_scales", align_bytes=64)
         w_raw = keep.tile([P, E + 1, 4, K], F32, name="w_raw")
-        w_bf = keep.tile([P, E, K, 4], BF16, name="w_bf", align_bytes=64)
+        w_bf = keep.tile([P, E + 1, K, 4], BF16, name="w_bf", align_bytes=64)
         w_codes = keep.tile([P, (E + 1) * K], U32, name="w_codes", align_bytes=64)
         w_scales = keep.tile([P, (E + 1) * K], U8, name="w_scales", align_bytes=64)
         gate_rows = keep.tile([P, P], F32, name="gate_rows")
@@ -49,7 +49,6 @@ def tile_moe_bds_lin_none_kernel(tc, dy_words, dy_scales, w, gate, offs, pos1, p
         made = keep.tile([P, P], F32, name="made")
         ident = keep.tile([P, P], F32, name="ident")
 
-        nc.gpsimd.memset(tok_scales[:].bitcast(I32), 0)
         make_identity(nc, made[:])
 
         def load_w(e0, e1):
@@ -58,22 +57,21 @@ def tile_moe_bds_lin_none_kernel(tc, dy_words, dy_scales, w, gate, offs, pos1, p
                 w[e0:e1].rearrange("e (p t) k -> p e (t k)", t=4),
             )
 
-        nc.sync.dma_start(offs_t[:], offs)
         for q in range(4):
-            queue = nc.sync if q < 2 else nc.scalar
-            queue.dma_start(tok_scales[32 * q : 32 * q + 4, :].bitcast(I32), dy_scales[0, 4 * q : 4 * q + 4, :].bitcast(I32))
+            rows = dy_scales[0, 4 * q : 4 * q + 4, :].bitcast(I32)
+            nc.sync.dma_start(tok_scales[32 * q : 32 * q + 32, :].bitcast(I32), rows.unsqueeze(0).to_broadcast([8, 4, T // 4]))
+        nc.sync.dma_start(offs_t[:], offs)
         nc.scalar.activation(ident[:], made[:], COPY)
         load_w(0, 1)
         load_w(1, 2)
         load_w(2, 4)
         load_w(4, 6)
         load_w(6, 8)
-        load_w(8, 10)
-        load_w(10, 12)
         nc.sync.dma_start(tok_words[:], dy_words[0].rearrange("p t d -> p (t d)").bitcast(I32))
+        load_w(8, 10)
+        load_w(10, 13)
         nc.sync.dma_start(gate_rows[:], gate.rearrange("k (b s) -> (k b) s", s=P)[0:P, :])
         nc.sync.dma_start(gate_tail[:], gate[:, TURNED * C :])
-        load_w(12, 13)
         for r, pos in enumerate((pos1, pos2, pos3)):
             nc.sync.dma_start(pos_t[r][:], pos)
 
@@ -104,10 +102,10 @@ def tile_moe_bds_lin_none_kernel(tc, dy_words, dy_scales, w, gate, offs, pos1, p
         for s0 in range(0, S, 768):
             nc.vector.tensor_copy(slot_scales[:, s0 : s0 + 768], tok_scales[:].indirect(offs_t[:, s0 // 16 : (s0 + 768) // 16]))
 
-        for e in range(E):
+        for e in range(E + 1):
             cast_w(e, w_bf[:, e])
-        for e0 in range(0, E, 4):
-            quantize_w(e0, e0 + 4, w_bf[:, e0 : e0 + 4].rearrange("p e k t -> p (e k t)"))
+        for e0, e1 in ((0, 4), (4, 8), (8, 12), (12, 13)):
+            quantize_w(e0, e1, w_bf[:, e0:e1].rearrange("p e k t -> p (e k t)"))
         gate_ps = psum.tile([P, BANK], F32, name="gate_ps", tag="sum")
         nc.tensor.transpose(gate_ps[:, 0:P], gate_rows[:], ident[:])
         nc.scalar.copy(gate_cols[:], gate_ps[:, 0 : 2 * TURNED])
@@ -150,9 +148,6 @@ def tile_moe_bds_lin_none_kernel(tc, dy_words, dy_scales, w, gate, offs, pos1, p
         apply_gate(10, 11, acc1)
         apply_gate(11, 12, acc2)
 
-        shared_bf = ring.tile([P, K, 4], BF16, name="shared_bf", tag="gated", align_bytes=64)
-        cast_w(E, shared_bf[:])
-        quantize_w(E, E + 1, shared_bf[:].rearrange("p k t -> p (k t)"))
         for h in range(2):
             cols = slice(h * BANK, (h + 1) * BANK)
             ds_ps = psum.tile([P, BANK], F32, name="ds_ps", tag="back")
@@ -174,19 +169,21 @@ def tile_moe_bds_lin_none_kernel(tc, dy_words, dy_scales, w, gate, offs, pos1, p
             add_turned(ds, h, True, False)
         for h in range(2):
             add_turned(picked[0], h, False, False)
+        by_token = keep.tile([P, T // P, K], F32, name="by_token")
         totals = []
         for h in range(2):
             pick(1, h * BANK, (h + 1) * BANK)
             add_turned(picked[1], h, False, True)
-            by_token = ring.tile([P, 4, K], F32, name="by_token")
-            nc.scalar.copy(by_token[:], sums[h][:])
-            total = psum.tile([P, BANK], F32, name="total", tag="total")
-            for j in range(4):
-                nc.tensor.transpose(total[:, j * P : (j + 1) * P], by_token[:, j, :], ident[:])
-            totals.append(total)
+            for u in range(2):
+                nc.scalar.copy(by_token[:, 4 * h + 2 * u : 4 * h + 2 * u + 2, :], sums[h][:, 2 * u : 2 * u + 2, :])
+                if h == 1 or u == 0:
+                    total = psum.tile([P, BANK], F32, name="total", tag=("total", "mx")[h])
+                    totals.append(total)
+                for j in range(2):
+                    c0 = (2 * u * (1 - h) + j) * P
+                    nc.tensor.transpose(total[:, c0 : c0 + P], by_token[:, 4 * h + 2 * u + j, :], ident[:])
         for h in range(2):
             pick(2, h * BANK, (h + 1) * BANK)
-        for t0, t1, queue in ((0, 512, nc.sync), (512, 768, nc.scalar), (768, 1024, nc.sync)):
-            h = t0 // BANK
-            nc.vector.tensor_tensor(result[:, t0:t1], picked[2][:, t0:t1], totals[h][:, t0 - h * BANK : t1 - h * BANK], ADD)
+        for i, (t0, t1, queue) in enumerate(((0, 512, nc.sync), (512, 768, nc.scalar), (768, 1024, nc.sync))):
+            nc.vector.tensor_tensor(result[:, t0:t1], picked[2][:, t0:t1], totals[i][:, 0 : t1 - t0], ADD)
             queue.dma_start(out[:, t0:t1], result[:, t0:t1])

@@ -35,9 +35,10 @@ def tile_moe_bds_lin_none_kernel(tc, dy_words, dy_scales, w, gate, offs, pos1, p
         tok_words = keep.tile([P, T], I32, name="tok_words", align_bytes=64)
         tok_scales = keep.tile([P, T], U8, name="tok_scales", align_bytes=64)
         slot_scales = keep.tile([P, S], U8, name="slot_scales", align_bytes=64)
-        w_raw = keep.tile([P, E + 1, 4, K], F32, name="w_raw")
+        w_raw = keep.tile([P, E - 1, 4, K], F32, name="w_raw")
+        late_raw = [ring.tile([P, 4, K], F32, name="late_raw%d" % i, tag="gated", align_bytes=64) for i in range(2)]
         w_bf = keep.tile([P, E + 1, K, 4], BF16, name="w_bf", align_bytes=64)
-        w_codes = keep.tile([P, (E + 1) * K], U32, name="w_codes", align_bytes=64)
+        w_codes = keep.tile([P, E * K], U32, name="w_codes", align_bytes=64)
         w_scales = keep.tile([P, (E + 1) * K], U8, name="w_scales", align_bytes=64)
         gate_rows = keep.tile([P, P], F32, name="gate_rows")
         gate_cols = keep.tile([P, 2 * TURNED], F32, name="gate_cols")
@@ -59,37 +60,39 @@ def tile_moe_bds_lin_none_kernel(tc, dy_words, dy_scales, w, gate, offs, pos1, p
 
         for q in range(4):
             rows = dy_scales[0, 4 * q : 4 * q + 4, :].bitcast(I32)
-            nc.sync.dma_start(tok_scales[32 * q : 32 * q + 32, :].bitcast(I32), rows.unsqueeze(0).to_broadcast([8, 4, T // 4]))
+            (nc.sync if q < 2 else nc.scalar).dma_start(tok_scales[32 * q : 32 * q + 32, :].bitcast(I32), rows.unsqueeze(0).to_broadcast([8, 4, T // 4]))
         nc.sync.dma_start(offs_t[:], offs)
         nc.scalar.activation(ident[:], made[:], COPY)
         load_w(0, 1)
         load_w(1, 2)
         load_w(2, 4)
+        nc.sync.dma_start(gate_rows[:], gate.rearrange("k (b s) -> (k b) s", s=P)[0:P, :])
         load_w(4, 6)
         load_w(6, 8)
         nc.sync.dma_start(tok_words[:], dy_words[0].rearrange("p t d -> p (t d)").bitcast(I32))
         load_w(8, 10)
-        load_w(10, 13)
-        nc.sync.dma_start(gate_rows[:], gate.rearrange("k (b s) -> (k b) s", s=P)[0:P, :])
+        load_w(10, 11)
+        for i in range(2):
+            nc.sync.dma_start(late_raw[i][:], w[E - 1 + i].rearrange("(p t) k -> p t k", t=4))
         nc.sync.dma_start(gate_tail[:], gate[:, TURNED * C :])
         for r, pos in enumerate((pos1, pos2, pos3)):
             nc.sync.dma_start(pos_t[r][:], pos)
 
-        def cast_w(e, dst):
+        def cast_w(e, src):
             nc.scalar.copy(
-                dst.rearrange("p (c i) t -> p c t i", i=4),
-                w_raw[:, e].rearrange("p t (c i) -> p c t i", i=4),
+                w_bf[:, e].rearrange("p (c i) t -> p c t i", i=4),
+                src.rearrange("p t (c i) -> p c t i", i=4),
             )
 
-        def quantize_w(e0, e1, src):
+        def quantize_w(e0, e1, codes):
             nc.vector.quantize_mx(
-                out=w_codes[:, e0 * K : e1 * K].bitcast(FP8X4),
+                out=codes.bitcast(FP8X4),
                 scales=w_scales[:, e0 * K : e1 * K],
-                in_=src,
+                in_=w_bf[:, e0:e1].rearrange("p e k t -> p (e k t)"),
             )
 
         def gather_words(s0, s1):
-            slot_words = ring.tile([P, BANK], U32, name="slot_words", align_bytes=64)
+            slot_words = ring.tile([P, BANK], U32, name="slot_words", tag="words", align_bytes=64)
             nc.vector.tensor_copy(slot_words[:, 0 : s1 - s0], tok_words[:].bitcast(U32).indirect(offs_t[:, s0 // 16 : s1 // 16]))
             return slot_words
 
@@ -103,9 +106,9 @@ def tile_moe_bds_lin_none_kernel(tc, dy_words, dy_scales, w, gate, offs, pos1, p
             nc.vector.tensor_copy(slot_scales[:, s0 : s0 + 768], tok_scales[:].indirect(offs_t[:, s0 // 16 : (s0 + 768) // 16]))
 
         for e in range(E + 1):
-            cast_w(e, w_bf[:, e])
-        for e0, e1 in ((0, 4), (4, 8), (8, 12), (12, 13)):
-            quantize_w(e0, e1, w_bf[:, e0:e1].rearrange("p e k t -> p (e k t)"))
+            cast_w(e, w_raw[:, e] if e < E - 1 else late_raw[e - E + 1][:])
+        for e0 in range(0, E, 4):
+            quantize_w(e0, e0 + 4, w_codes[:, e0 * K : (e0 + 4) * K])
         gate_ps = psum.tile([P, BANK], F32, name="gate_ps", tag="sum")
         nc.tensor.transpose(gate_ps[:, 0:P], gate_rows[:], ident[:])
         nc.scalar.copy(gate_cols[:], gate_ps[:, 0 : 2 * TURNED])
@@ -128,9 +131,9 @@ def tile_moe_bds_lin_none_kernel(tc, dy_words, dy_scales, w, gate, offs, pos1, p
                 nc.tensor.transpose(back[:, j * P : (j + 1) * P], gated[:, j, :], ident[:])
             nc.scalar.copy(dx[:, s0 : s0 + BANK], back[:])
 
-        def multiply(e0, e1):
+        def multiply(e0, e1, tag):
             words = gather_words(e0 * C, e1 * C)
-            acc = psum.tile([P, BANK], F32, name="acc", tag="mx")
+            acc = psum.tile([P, BANK], F32, name="acc", tag=tag)
             for e in range(e0, e1):
                 cols = slice((e - e0) * C, (e - e0 + 1) * C)
                 mx(acc[:, cols], w_codes[:, e * K : (e + 1) * K], w_scales[:, e * K : (e + 1) * K],
@@ -141,17 +144,19 @@ def tile_moe_bds_lin_none_kernel(tc, dy_words, dy_scales, w, gate, offs, pos1, p
             nc.vector.tensor_tensor(dx[:, e0 * C : e1 * C], acc[:, 0 : (e1 - e0) * C],
                                     gate_tail[:, (e0 - TURNED) * C : (e1 - TURNED) * C], MULT)
 
-        acc0 = multiply(8, 10)
-        acc1 = multiply(10, 11)
-        apply_gate(8, 10, acc0)
-        acc2 = multiply(11, 12)
-        apply_gate(10, 11, acc1)
+        acc0 = multiply(8, 9, "mx")
+        acc1 = multiply(9, 11, "mx")
+        acc2 = multiply(11, 12, "back")
+        apply_gate(8, 9, acc0)
+        apply_gate(9, 11, acc1)
         apply_gate(11, 12, acc2)
+        shared_codes = ring.tile([P, K], U32, name="shared_codes", tag="words", align_bytes=64)
+        quantize_w(E, E + 1, shared_codes[:])
 
         for h in range(2):
             cols = slice(h * BANK, (h + 1) * BANK)
             ds_ps = psum.tile([P, BANK], F32, name="ds_ps", tag="back")
-            mx(ds_ps[:], w_codes[:, E * K :], w_scales[:, E * K :], tok_words[:, cols], tok_scales[:, cols])
+            mx(ds_ps[:], shared_codes[:], w_scales[:, E * K :], tok_words[:, cols], tok_scales[:, cols])
             nc.scalar.copy(ds[:, cols], ds_ps[:])
 
         def pick(r, t0, t1):

from contextlib import ExitStack

import concourse.mybir as mybir
from concourse.masks import make_identity

K, T, E, C, N = 128, 1024, 12, 256, 512
S = E * C
P = 128
FLOPS = 2 * N * K * (S + T)

F32 = mybir.dt.float32
BF16 = mybir.dt.bfloat16
I32 = mybir.dt.int32
U32 = mybir.dt.uint32
U16 = mybir.dt.uint16
U8 = mybir.dt.uint8
FP8X4 = mybir.dt.float8_e4m3fn_x4
COPY = mybir.ActivationFunctionType.Copy
MULT = mybir.AluOpType.mult
ADD = mybir.AluOpType.add

BANK = 512
TURNED = 8


def tile_moe_bds_lin_none_kernel(tc, dy_words, dy_scales, w, gate, offs, pos1, pos2, pos3, out):
    nc = tc.nc
    with ExitStack() as ctx:
        keep = ctx.enter_context(tc.tile_pool(name="keep", bufs=1))
        ring = ctx.enter_context(tc.tile_pool(name="ring", bufs=2))
        psum = ctx.enter_context(tc.psum_pool(name="psum", bufs=2))

        offs_t = keep.tile([P, S // 16], U16, name="offs_t")
        pos_t = [keep.tile([P, T // 16], U16, name="pos%d_t" % r) for r in range(3)]
        tok_words = keep.tile([P, T], I32, name="tok_words", align_bytes=64)
        tok_scales = keep.tile([P, T], U8, name="tok_scales", align_bytes=64)
        slot_scales = keep.tile([P, S], U8, name="slot_scales", align_bytes=64)
        w_raw = keep.tile([P, E - 1, 4, K], F32, name="w_raw")
        late_raw = [ring.tile([P, 4, K], F32, name="late_raw%d" % i, tag="gated", align_bytes=64) for i in range(2)]
        w_bf = keep.tile([P, E + 1, K, 4], BF16, name="w_bf", align_bytes=64)
        w_codes = keep.tile([P, E * K], U32, name="w_codes", align_bytes=64)
        w_scales = keep.tile([P, (E + 1) * K], U8, name="w_scales", align_bytes=64)
        gate_rows = keep.tile([P, P], F32, name="gate_rows")
        gate_cols = keep.tile([P, 2 * TURNED], F32, name="gate_cols")
        gate_tail = keep.tile([P, (E - TURNED) * C], F32, name="gate_tail")
        dx = keep.tile([P, S], F32, name="dx")
        ds = keep.tile([P, T], F32, name="ds")
        picked = [keep.tile([P, T], F32, name="picked%d" % r) for r in range(3)]
        result = keep.tile([P, T], F32, name="result")
        made = keep.tile([P, P], F32, name="made")
        ident = keep.tile([P, P], F32, name="ident")

        make_identity(nc, made[:])

        def load_w(e0, e1):
            nc.sync.dma_start(
                w_raw[:, e0:e1].rearrange("p e t k -> p e (t k)"),
                w[e0:e1].rearrange("e (p t) k -> p e (t k)", t=4),
            )

        for q in range(4):
            rows = dy_scales[0, 4 * q : 4 * q + 4, :].bitcast(I32)
            (nc.sync if q < 2 else nc.scalar).dma_start(tok_scales[32 * q : 32 * q + 32, :].bitcast(I32), rows.unsqueeze(0).to_broadcast([8, 4, T // 4]))
        nc.sync.dma_start(offs_t[:], offs)
        nc.scalar.activation(ident[:], made[:], COPY)
        load_w(0, 1)
        load_w(1, 2)
        load_w(2, 4)
        nc.sync.dma_start(gate_rows[:], gate.rearrange("k (b s) -> (k b) s", s=P)[0:P, :])
        load_w(4, 6)
        load_w(6, 8)
        nc.sync.dma_start(tok_words[:], dy_words[0].rearrange("p t d -> p (t d)").bitcast(I32))
        load_w(8, 10)
        load_w(10, 11)
        for i in range(2):
            nc.sync.dma_start(late_raw[i][:], w[E - 1 + i].rearrange("(p t) k -> p t k", t=4))
        nc.sync.dma_start(gate_tail[:], gate[:, TURNED * C :])
        for r, pos in enumerate((pos1, pos2, pos3)):
            nc.sync.dma_start(pos_t[r][:], pos)

        def cast_w(e, src):
            nc.scalar.copy(
                w_bf[:, e].rearrange("p (c i) t -> p c t i", i=4),
                src.rearrange("p t (c i) -> p c t i", i=4),
            )

        def quantize_w(e0, e1, codes):
            nc.vector.quantize_mx(
                out=codes.bitcast(FP8X4),
                scales=w_scales[:, e0 * K : e1 * K],
                in_=w_bf[:, e0:e1].rearrange("p e k t -> p (e k t)"),
            )

        def gather_words(s0, s1):
            slot_words = ring.tile([P, BANK], U32, name="slot_words", tag="words", align_bytes=64)
            nc.vector.tensor_copy(slot_words[:, 0 : s1 - s0], tok_words[:].bitcast(U32).indirect(offs_t[:, s0 // 16 : s1 // 16]))
            return slot_words

        def mx(acc, lhs_words, lhs_scales, rhs_words, rhs_scales):
            nc.tensor.matmul_mx(
                out=acc, lhsT=lhs_words.bitcast(FP8X4), lhsT_scale=lhs_scales,
                rhs=rhs_words.bitcast(FP8X4), rhs_scale=rhs_scales, start=True, stop=True,
            )

        for s0 in range(0, S, 768):
            nc.vector.tensor_copy(slot_scales[:, s0 : s0 + 768], tok_scales[:].indirect(offs_t[:, s0 // 16 : (s0 + 768) // 16]))

        for e in range(E + 1):
            cast_w(e, w_raw[:, e] if e < E - 1 else late_raw[e - E + 1][:])
        for e0 in range(0, E, 4):
            quantize_w(e0, e0 + 4, w_codes[:, e0 * K : (e0 + 4) * K])
        gate_ps = psum.tile([P, BANK], F32, name="gate_ps", tag="sum")
        nc.tensor.transpose(gate_ps[:, 0:P], gate_rows[:], ident[:])
        nc.scalar.copy(gate_cols[:], gate_ps[:, 0 : 2 * TURNED])

        for c in range(TURNED // 2):
            s0 = c * BANK
            words = gather_words(s0, s0 + BANK)
            by_slot = psum.tile([P, 4, K], F32, name="by_slot", tag="mx")
            for j in range(4):
                b = 4 * c + j
                e = b // 2
                mx(by_slot[:, j, :], words[:, j * P : (j + 1) * P], slot_scales[:, b * P : (b + 1) * P],
                   w_codes[:, e * K : (e + 1) * K], w_scales[:, e * K : (e + 1) * K])
            gated = ring.tile([P, 4, K], F32, name="gated", tag="gated", align_bytes=64)
            for j in range(4):
                b = 4 * c + j
                nc.scalar.activation(gated[:, j, :], by_slot[:, j, :], COPY, scale=gate_cols[:, b : b + 1])
            back = psum.tile([P, BANK], F32, name="back", tag="back")
            for j in range(4):
                nc.tensor.transpose(back[:, j * P : (j + 1) * P], gated[:, j, :], ident[:])
            nc.scalar.copy(dx[:, s0 : s0 + BANK], back[:])

        def multiply(e0, e1, tag):
            words = gather_words(e0 * C, e1 * C)
            acc = psum.tile([P, BANK], F32, name="acc", tag=tag)
            for e in range(e0, e1):
                cols = slice((e - e0) * C, (e - e0 + 1) * C)
                mx(acc[:, cols], w_codes[:, e * K : (e + 1) * K], w_scales[:, e * K : (e + 1) * K],
                   words[:, cols], slot_scales[:, e * C : (e + 1) * C])
            return acc

        def apply_gate(e0, e1, acc):
            nc.vector.tensor_tensor(dx[:, e0 * C : e1 * C], acc[:, 0 : (e1 - e0) * C],
                                    gate_tail[:, (e0 - TURNED) * C : (e1 - TURNED) * C], MULT)

        acc0 = multiply(8, 9, "mx")
        acc1 = multiply(9, 11, "mx")
        acc2 = multiply(11, 12, "back")
        apply_gate(8, 9, acc0)
        apply_gate(9, 11, acc1)
        apply_gate(11, 12, acc2)
        shared_codes = ring.tile([P, K], U32, name="shared_codes", tag="words", align_bytes=64)
        quantize_w(E, E + 1, shared_codes[:])

        for h in range(2):
            cols = slice(h * BANK, (h + 1) * BANK)
            ds_ps = psum.tile([P, BANK], F32, name="ds_ps", tag="back")
            mx(ds_ps[:], shared_codes[:], w_scales[:, E * K :], tok_words[:, cols], tok_scales[:, cols])
            nc.scalar.copy(ds[:, cols], ds_ps[:])

        def pick(r, t0, t1):
            nc.vector.tensor_copy(picked[r][:, t0:t1], dx[:].indirect(pos_t[r][:, t0 // 16 : t1 // 16]))

        sums = [psum.tile([P, 4, K], F32, name="sum%d" % h, tag="sum") for h in range(2)]

        def add_turned(src, h, first, last):
            for j in range(4):
                t0 = h * BANK + j * P
                nc.tensor.matmul(sums[h][:, j, :], src[:, t0 : t0 + P], ident[:], start=(first and j == 0), stop=(last and j == 3), is_transpose=True)

        pick(0, 0, T)
        for h in range(2):
            add_turned(ds, h, True, False)
        for h in range(2):
            add_turned(picked[0], h, False, False)
        by_token = keep.tile([P, T // P, K], F32, name="by_token")
        totals = []
        for h in range(2):
            pick(1, h * BANK, (h + 1) * BANK)
            add_turned(picked[1], h, False, True)
            for u in range(2):
                nc.scalar.copy(by_token[:, 4 * h + 2 * u : 4 * h + 2 * u + 2, :], sums[h][:, 2 * u : 2 * u + 2, :])
                if h == 1 or u == 0:
                    total = psum.tile([P, BANK], F32, name="total", tag=("total", "mx")[h])
                    totals.append(total)
                for j in range(2):
                    c0 = (2 * u * (1 - h) + j) * P
                    nc.tensor.transpose(total[:, c0 : c0 + P], by_token[:, 4 * h + 2 * u + j, :], ident[:])
        for h in range(2):
            pick(2, h * BANK, (h + 1) * BANK)
        for i, (t0, t1, queue) in enumerate(((0, 512, nc.sync), (512, 768, nc.scalar), (768, 1024, nc.sync))):
            nc.vector.tensor_tensor(result[:, t0:t1], picked[2][:, t0:t1], totals[i][:, 0 : t1 - t0], ADD)
            queue.dma_start(out[:, t0:t1], result[:, t0:t1])
